import numpy as np
import ml_dtypes


def mxq(x, axis, fmt="e4m3"):
    dtype, down = {"e4m3": (ml_dtypes.float8_e4m3fn, 7), "e5m2": (ml_dtypes.float8_e5m2, 14)}[fmt]
    v = np.moveaxis(np.asarray(x, np.float32).astype(ml_dtypes.bfloat16).astype(np.float64), axis, -1)
    blocks = v.reshape(v.shape[:-1] + (-1, 32))
    amax = np.abs(blocks).max(-1, keepdims=True)
    byte = np.maximum(np.where(amax > 0, np.frexp(amax)[1] - 1 + 127, 0) - down, 1)
    scale = np.exp2(byte - 127.0)
    codes = (blocks / scale).astype(np.float32).astype(dtype).astype(np.float64)
    return np.moveaxis((codes * scale).reshape(v.shape), -1, axis)


WIDE = False


def mx_kscale(k, group=512):
    if not WIDE:
        return np.ones(k)
    levels = np.array([10, -10, 5, -5, 0])
    if group != 512:
        return np.exp2(np.random.permutation(np.resize(levels, k // group))).repeat(group)
    if k % 512:
        return np.exp2(np.random.permutation(np.resize(levels, k // 32))).repeat(32)
    a = np.empty((k // 512, 16))
    for p in range(k // 512):
        a[p, :8] = np.random.permutation(np.resize(levels, 8))
        for g in range(8):
            far = levels[np.abs(levels - a[p, g]) >= 10]
            a[p, g + 8] = far[np.random.randint(len(far))]
    return np.exp2(a.ravel()).repeat(32)


def f64(x):
    return np.asarray(x).astype(np.float64)


def striped(idx):
    return np.tile(np.asarray(idx).reshape(-1, 16).T, (8, 1)).astype(np.uint16)


def unstriped(offs):
    return offs[:16].T.reshape(-1).astype(np.int64)


H, KV, D, NQ, N = 2, 2, 256, 512, 512


def setup_inputs():
    n = np.random.standard_normal
    s = mx_kscale(D, 0)[:, None]
    u = mx_kscale(N)
    t = np.random.uniform(0.5, 2.0, N) * u
    v = n((KV, N, 128))
    v[:, :, 127] = 1.0
    return {
        "qT": (n((H, D, NQ)) * s * (0.70 / np.sqrt(D))).astype(np.float32),
        "kT": (n((KV, D, N)) / s).astype(np.float32),
        "t": t.reshape(N, 1).astype(np.float32),
        "v": (v / t[:, None]).astype(np.float32),
        "kb": (0.5 * n((N, 1))).astype(np.float32),
        "og": n((H, NQ, 128)).astype(np.float32),
    }


def reference(qT, kT, t, v, kb, og):
    a = mxq(f64(kT), 1, "e4m3").transpose(0, 2, 1) @ mxq(f64(qT), 1, "e4m3")
    a = a + f64(kb)
    p = np.square(np.maximum(a, 0.0))
    w = p * f64(t)
    y = mxq(w, 1, "e4m3").transpose(0, 2, 1) @ mxq(f64(v), 1, "e4m3")
    y = y / (y[:, :, 127:128] + 1.0)
    y = y / (1.0 + np.exp(-f64(og)))
    return y

@@ -1,0 +1,239 @@
+from contextlib import ExitStack
+
+import concourse.mybir as mybir
+
+H, D, NQ, N, E = 2, 256, 512, 512, 128
+FLOPS = 2 * H * NQ * N * (D + E)
+
+F32 = mybir.dt.float32
+BF16 = mybir.dt.bfloat16
+U32 = mybir.dt.uint32
+U8 = mybir.dt.uint8
+FP8X4 = mybir.dt.float8_e4m3fn_x4
+ACT = mybir.ActivationFunctionType
+ALU = mybir.AluOpType
+
+P = 128
+PACK = 4
+ROWS = D // PACK
+HALF = NQ // 2
+TILES = HALF // P
+Q_SPLIT = 84
+
+
+def tile_rows_a_relu2_kb_gate_kernel(tc, qT, kT, t, v, kb, og, out):
+    nc = tc.nc
+    with ExitStack() as ctx:
+        sb = ctx.enter_context(tc.tile_pool(name="sb", bufs=1))
+        ps = ctx.enter_context(tc.psum_pool(name="ps", bufs=1))
+        ctx.enter_context(tc.manual_schedule())
+
+        def tile(name, shape, dtype):
+            return sb.tile(shape, dtype, name=name, align_bytes=64)
+
+        def quantize(name, grouped):
+            width = grouped.shape[1] // PACK
+            codes = tile(name + "_codes", [P, width], U32)
+            scales = tile(name + "_scales", [P, width], U8)
+            nc.vector.quantize_mx(out=codes[:].bitcast(FP8X4), scales=scales[:], in_=grouped)
+            return codes, scales
+
+        units = [(half, h) for half in range(2) for h in range(H)]
+
+        t_sb = tile("t_sb", [P, PACK], F32)
+        kb_sb = tile("kb_sb", [P, PACK], F32)
+        og_sb = [tile("og_sb%d" % u, [P, TILES * E], F32) for u in range(len(units))]
+        k_raw = tile("k_raw", [P, PACK, N], F32)
+        q_raw = [tile("q_raw%d" % half, [P, PACK, HALF], F32) for half in range(2)]
+        v_raw = tile("v_raw", [P, H, PACK * E], F32)
+
+        def og_rows(ap, u):
+            half, h = units[u]
+            return ap[h, half * HALF : (half + 1) * HALF, :].rearrange("(p m) e -> p (m e)", m=TILES)
+
+        q_view = qT.rearrange("h (p j) n -> (h p) j n", j=PACK)
+        nc.sync.dma_start(out=t_sb[:], in_=t.rearrange("(p j) o -> p (j o)", j=PACK))
+        nc.scalar.dma_start(out=kb_sb[:], in_=kb.rearrange("(p j) o -> p (j o)", j=PACK))
+        nc.sync.dma_start(out=k_raw[:], in_=kT.rearrange("h (p j) n -> (h p) j n", j=PACK))
+        nc.scalar.dma_start(out=og_sb[0][:], in_=og_rows(og, 0))
+        for half in range(2):
+            nc.sync.dma_start(out=q_raw[half][:], in_=q_view[:, :, half * HALF : (half + 1) * HALF])
+        nc.sync.dma_start(out=v_raw[:], in_=v.rearrange("h (p j) e -> p h (j e)", j=PACK))
+        for u in range(1, len(units)):
+            nc.sync.dma_start(out=og_sb[u][:], in_=og_rows(og, u))
+
+        half_const = tile("half_const", [P, PACK], F32)
+        nc.gpsimd.memset(half_const[:], 0.5)
+        t_abs = tile("t_abs", [P, PACK], F32)
+        t_pos = tile("t_pos", [P, PACK], F32)
+        t_sign = tile("t_sign", [P, PACK], F32)
+        root = tile("root", [P, PACK], F32)
+        root_kb = tile("root_kb", [P, PACK], F32)
+        nc.vector.scalar_tensor_tensor(out=t_abs[:], in0=t_sb[:], scalar=-1.0, in1=t_sb[:], op0=ALU.mult, op1=ALU.max)
+        nc.vector.tensor_scalar(out=t_pos[:], in0=t_sb[:], scalar1=0.0, scalar2=2.0, op0=ALU.is_ge, op1=ALU.mult)
+        nc.vector.tensor_scalar(out=t_sign[:], in0=t_pos[:], scalar1=-1.0, scalar2=None, op0=ALU.add)
+        nc.gpsimd.tensor_tensor(out=root[:], in0=t_abs[:], in1=half_const[:], op=ALU.pow)
+        nc.gpsimd.tensor_tensor(out=root_kb[:], in0=root[:], in1=kb_sb[:], op=ALU.mult)
+
+        gate = [tile("gate%d" % u, [P, TILES * E], F32) for u in range(len(units))]
+
+        def sigmoid(u):
+            nc.scalar.activation(out=gate[u][:], in_=og_sb[u][:], func=ACT.Sigmoid)
+
+        k_grouped = [tile("k_grouped%d" % rp, [P, 2 * P * PACK], BF16) for rp in range(2)]
+
+        def group_k(rp, copy):
+            copy(
+                out=k_grouped[rp][:].rearrange("p (r s j) -> p s j r", r=2, j=PACK),
+                in_=k_raw[:].rearrange("p j (s r) -> p s j r", r=PACK)[:, :, :, 2 * rp : 2 * rp + 2],
+            )
+
+        q_grouped = [tile("q_grouped%d" % half, [P, HALF * PACK], BF16) for half in range(2)]
+
+        def group_q(half, s0, s1, copy):
+            copy(
+                out=q_grouped[half][:].rearrange("p (m s j) -> p s j m", m=TILES, j=PACK)[:, s0:s1],
+                in_=q_raw[half][:].rearrange("p j (s m) -> p s j m", m=TILES)[:, s0:s1],
+            )
+
+        v_grouped = tile("v_grouped", [P, H * E * PACK], BF16)
+
+        def group_v(h):
+            nc.vector.tensor_tensor(
+                out=v_grouped[:, h * E * PACK : (h + 1) * E * PACK].rearrange("p (c i j) -> p c j i", i=2, j=PACK),
+                in0=v_raw[:, h, :].rearrange("p (j c i) -> p c j i", i=2, j=PACK),
+                in1=t_sign[:].unsqueeze(1).unsqueeze(3).to_broadcast([P, E // 2, PACK, 2]),
+                op=ALU.mult,
+            )
+
+        k_mx = {}
+        q_mx = {}
+        w_mx = {}
+        rect = [tile("rect%d" % u, [P, PACK, HALF], F32) for u in range(len(units))]
+        w_grouped = [[tile("w_grouped%d_%d" % (u, m), [P, P * PACK], BF16) for m in range(TILES)] for u in range(len(units))]
+        y_ps = {}
+        den = [tile("den%d" % u, [P, TILES], F32) for u in range(len(units))]
+        rden = [tile("rden%d" % u, [P, TILES], F32) for u in range(len(units))]
+        res = [[tile("res%d_%d" % (u, m), [P, E], F32) for m in range(TILES)] for u in range(len(units))]
+
+        def scores(u, r):
+            half, h = units[u]
+            rows = slice(h * ROWS, (h + 1) * ROWS)
+            kc, ks = k_mx[r // 2]
+            qc, qs = q_mx[half]
+            kcols = slice((r % 2) * P, (r % 2 + 1) * P)
+            bank = ps.tile([P, HALF], F32, name="score_bank", tag="score%d" % h, bufs=3)
+            for m in range(TILES):
+                qcols = slice(m * P, (m + 1) * P)
+                nc.tensor.matmul_mx(
+                    out=bank[:, qcols],
+                    lhsT=kc[rows, kcols].bitcast(FP8X4),
+                    lhsT_scale=ks[rows, kcols],
+                    rhs=qc[rows, qcols].bitcast(FP8X4),
+                    rhs_scale=qs[rows, qcols],
+                    start=True,
+                    stop=True,
+                )
+            nc.scalar.activation(
+                out=rect[u][:, r, :], in_=bank[:], func=ACT.Relu,
+                bias=root_kb[:, r : r + 1], scale=root[:, r : r + 1],
+            )
+
+        def square(u, m, on_scalar):
+            src = rect[u][:, :, m * P : (m + 1) * P].rearrange("p r (c i) -> p c r i", i=2)
+            dst = w_grouped[u][m][:].rearrange("p (c i r) -> p c r i", i=2, r=PACK)
+            if on_scalar:
+                nc.scalar.activation(out=dst, in_=src, func=ACT.Square)
+            else:
+                nc.vector.tensor_tensor(out=dst, in0=src, in1=src, op=ALU.mult)
+
+        def quant_w(u, m):
+            w_mx[u, m] = quantize("w%d_%d" % (u, m), w_grouped[u][m][:])
+
+        def second(u):
+            half, h = units[u]
+            vc, vs = v_mx[0]
+            y_ps[u] = ps.tile([P, TILES, E], F32, name="y_bank", tag="y", bufs=2)
+            for m in range(TILES):
+                wc, ws = w_mx[u, m]
+                nc.tensor.matmul_mx(
+                    out=y_ps[u][:, m, :],
+                    lhsT=wc[:].bitcast(FP8X4),
+                    lhsT_scale=ws[:],
+                    rhs=vc[:, h * E : (h + 1) * E].bitcast(FP8X4),
+                    rhs_scale=vs[:, h * E : (h + 1) * E],
+                    start=True,
+                    stop=True,
+                )
+
+        def den_add(u):
+            nc.vector.tensor_scalar(out=den[u][:], in0=y_ps[u][:, :, E - 1], scalar1=1.0, scalar2=None, op0=ALU.add)
+
+        def den_recip(u):
+            nc.vector.reciprocal(out=rden[u][:], in_=den[u][:])
+
+        def finish(u, m, queue):
+            half, h = units[u]
+            nc.vector.scalar_tensor_tensor(
+                out=res[u][m][:], in0=y_ps[u][:, m, :], scalar=rden[u][:, m : m + 1],
+                in1=gate[u][:, m * E : (m + 1) * E], op0=ALU.mult, op1=ALU.mult,
+            )
+            queue.dma_start(out=og_rows(out, u)[:, m * E : (m + 1) * E], in_=res[u][m][:])
+
+        v_mx = []
+        sigmoid(0)
+        group_k(0, nc.vector.tensor_copy)
+        group_k(1, nc.scalar.copy)
+        k_mx[0] = quantize("k0", k_grouped[0][:])
+        group_q(0, 0, Q_SPLIT, nc.vector.tensor_copy)
+        group_q(0, Q_SPLIT, P, nc.scalar.copy)
+        k_mx[1] = quantize("k1", k_grouped[1][:])
+        q_mx[0] = quantize("q0", q_grouped[0][:])
+        for r in range(PACK): scores(0, r)
+        group_q(1, 0, P, nc.vector.tensor_copy)
+        group_v(0)
+        q_mx[1] = quantize("q1", q_grouped[1][:])
+        group_v(1)
+        for r in range(PACK): scores(1, r)
+        square(0, 0, False)
+        v_mx.append(quantize("v", v_grouped[:]))
+        square(0, 1, False)
+        quant_w(0, 0)
+        for r in range(PACK): scores(2, r)
+        square(1, 0, False)
+        quant_w(0, 1)
+        second(0)
+        square(1, 1, False)
+        quant_w(1, 0)
+        sigmoid(1)
+        den_add(0)
+        quant_w(1, 1)
+        den_recip(0)
+        for r in range(PACK): scores(3, r)
+        second(1)
+        square(2, 0, False)
+        finish(0, 0, nc.sync)
+        finish(0, 1, nc.sync)
+        square(2, 1, True)
+        den_add(1)
+        quant_w(2, 0)
+        den_recip(1)
+        square(3, 0, True)
+        quant_w(2, 1)
+        second(2)
+        finish(1, 0, nc.sync)
+        finish(1, 1, nc.sync)
+        square(3, 1, True)
+        sigmoid(2)
+        sigmoid(3)
+        den_add(2)
+        quant_w(3, 0)
+        den_recip(2)
+        quant_w(3, 1)
+        second(3)
+        finish(2, 0, nc.sync)
+        finish(2, 1, nc.sync)
+        den_add(3)
+        den_recip(3)
+        finish(3, 0, nc.sync)
+        finish(3, 1, nc.scalar)

@@ -18,7 +18,7 @@ PACK = 4
 ROWS = D // PACK
 HALF = NQ // 2
 TILES = HALF // P
-Q_SPLIT = 84
+Q_SPLIT = 88
 
 
 def tile_rows_a_relu2_kb_gate_kernel(tc, qT, kT, t, v, kb, og, out):
@@ -53,12 +53,14 @@ def tile_rows_a_relu2_kb_gate_kernel(tc, qT, kT, t, v, kb, og, out):
 
         q_view = qT.rearrange("h (p j) n -> (h p) j n", j=PACK)
         nc.sync.dma_start(out=t_sb[:], in_=t.rearrange("(p j) o -> p (j o)", j=PACK))
+        og_first = tile("og_first", [P, E], F32)
+        nc.scalar.dma_start(out=og_first[:], in_=og_rows(og, 0)[:, :E])
         nc.scalar.dma_start(out=kb_sb[:], in_=kb.rearrange("(p j) o -> p (j o)", j=PACK))
         nc.sync.dma_start(out=k_raw[:], in_=kT.rearrange("h (p j) n -> (h p) j n", j=PACK))
-        nc.scalar.dma_start(out=og_sb[0][:], in_=og_rows(og, 0))
-        for half in range(2):
-            nc.sync.dma_start(out=q_raw[half][:], in_=q_view[:, :, half * HALF : (half + 1) * HALF])
+        nc.sync.dma_start(out=q_raw[0][:], in_=q_view[:, :, :HALF])
         nc.sync.dma_start(out=v_raw[:], in_=v.rearrange("h (p j) e -> p h (j e)", j=PACK))
+        nc.sync.dma_start(out=q_raw[1][:], in_=q_view[:, :, HALF:])
+        nc.sync.dma_start(out=og_sb[0][:, E:], in_=og_rows(og, 0)[:, E:])
         for u in range(1, len(units)):
             nc.sync.dma_start(out=og_sb[u][:], in_=og_rows(og, u))
 
@@ -77,8 +79,11 @@ def tile_rows_a_relu2_kb_gate_kernel(tc, qT, kT, t, v, kb, og, out):
 
         gate = [tile("gate%d" % u, [P, TILES * E], F32) for u in range(len(units))]
 
-        def sigmoid(u):
-            nc.scalar.activation(out=gate[u][:], in_=og_sb[u][:], func=ACT.Sigmoid)
+        def sigmoid(u, m0=0, m1=TILES):
+            src = og_first[:] if m1 == 1 else og_sb[u][:, m0 * E : m1 * E]
+            nc.scalar.activation(out=gate[u][:, m0 * E : m1 * E], in_=src, func=ACT.Sigmoid)
+
+        V, S = nc.vector.tensor_copy, nc.scalar.copy
 
         k_grouped = [tile("k_grouped%d" % rp, [P, 2 * P * PACK], BF16) for rp in range(2)]
 
@@ -90,7 +95,7 @@ def tile_rows_a_relu2_kb_gate_kernel(tc, qT, kT, t, v, kb, og, out):
 
         q_grouped = [tile("q_grouped%d" % half, [P, HALF * PACK], BF16) for half in range(2)]
 
-        def group_q(half, s0, s1, copy):
+        def group_q(half, copy, s0=0, s1=P):
             copy(
                 out=q_grouped[half][:].rearrange("p (m s j) -> p s j m", m=TILES, j=PACK)[:, s0:s1],
                 in_=q_raw[half][:].rearrange("p j (s m) -> p s j m", m=TILES)[:, s0:s1],
@@ -110,130 +115,165 @@ def tile_rows_a_relu2_kb_gate_kernel(tc, qT, kT, t, v, kb, og, out):
         q_mx = {}
         w_mx = {}
         rect = [tile("rect%d" % u, [P, PACK, HALF], F32) for u in range(len(units))]
-        w_grouped = [[tile("w_grouped%d_%d" % (u, m), [P, P * PACK], BF16) for m in range(TILES)] for u in range(len(units))]
-        y_ps = {}
-        den = [tile("den%d" % u, [P, TILES], F32) for u in range(len(units))]
-        rden = [tile("rden%d" % u, [P, TILES], F32) for u in range(len(units))]
-        res = [[tile("res%d_%d" % (u, m), [P, E], F32) for m in range(TILES)] for u in range(len(units))]
+        w_grouped = [tile("w_grouped%d" % u, [P, TILES * P * PACK], BF16) for u in range(len(units))]
+        res = [tile("res%d" % u, [P, TILES * E], F32) for u in range(len(units))]
 
-        def scores(u, r):
+        banks = {}
+
+        def full_scores(u):
             half, h = units[u]
             rows = slice(h * ROWS, (h + 1) * ROWS)
-            kc, ks = k_mx[r // 2]
             qc, qs = q_mx[half]
-            kcols = slice((r % 2) * P, (r % 2 + 1) * P)
-            bank = ps.tile([P, HALF], F32, name="score_bank", tag="score%d" % h, bufs=3)
-            for m in range(TILES):
-                qcols = slice(m * P, (m + 1) * P)
-                nc.tensor.matmul_mx(
-                    out=bank[:, qcols],
-                    lhsT=kc[rows, kcols].bitcast(FP8X4),
-                    lhsT_scale=ks[rows, kcols],
-                    rhs=qc[rows, qcols].bitcast(FP8X4),
-                    rhs_scale=qs[rows, qcols],
-                    start=True,
-                    stop=True,
-                )
-            nc.scalar.activation(
-                out=rect[u][:, r, :], in_=bank[:], func=ACT.Relu,
-                bias=root_kb[:, r : r + 1], scale=root[:, r : r + 1],
-            )
+            for rp in range(2):
+                kc, ks = k_mx[rp]
+                banks[u, rp] = ps.tile([P, 2, HALF], F32, name="score_bank", tag="score%d" % h, bufs=2)
+                for i in range(2):
+                    kcols = slice(i * P, (i + 1) * P)
+                    for m in range(TILES):
+                        qcols = slice(m * P, (m + 1) * P)
+                        nc.tensor.matmul_mx(
+                            out=banks[u, rp][:, i, qcols],
+                            lhsT=kc[rows, kcols].bitcast(FP8X4),
+                            lhsT_scale=ks[rows, kcols],
+                            rhs=qc[rows, qcols].bitcast(FP8X4),
+                            rhs_scale=qs[rows, qcols],
+                            start=True,
+                            stop=True,
+                        )
 
-        def square(u, m, on_scalar):
+        def full_rect(u):
+            for r in range(PACK):
+                nc.scalar.activation(
+                    out=rect[u][:, r, :], in_=banks[u, r // 2][:, r % 2, :], func=ACT.Relu,
+                    bias=root_kb[:, r : r + 1], scale=root[:, r : r + 1],
+                )
+
+        def quant_k(rp):
+            k_mx[rp] = quantize("k%d" % rp, k_grouped[rp][:])
+
+        def quant_q(half):
+            q_mx[half] = quantize("q%d" % half, q_grouped[half][:])
+
+        def quant_v():
+            v_mx.append(quantize("v", v_grouped[:]))
+
+        def square(u, m, eng):
             src = rect[u][:, :, m * P : (m + 1) * P].rearrange("p r (c i) -> p c r i", i=2)
-            dst = w_grouped[u][m][:].rearrange("p (c i r) -> p c r i", i=2, r=PACK)
-            if on_scalar:
+            dst = w_grouped[u][:, m * P * PACK : (m + 1) * P * PACK].rearrange("p (c i r) -> p c r i", i=2, r=PACK)
+            if eng is S:
                 nc.scalar.activation(out=dst, in_=src, func=ACT.Square)
             else:
                 nc.vector.tensor_tensor(out=dst, in0=src, in1=src, op=ALU.mult)
 
-        def quant_w(u, m):
-            w_mx[u, m] = quantize("w%d_%d" % (u, m), w_grouped[u][m][:])
+        def quant_w(*tiles):
+            u, m0 = tiles[0]
+            wc, ws = quantize("w%d_%d" % (u, m0), w_grouped[u][:, m0 * P * PACK : (m0 + len(tiles)) * P * PACK])
+            for i, um in enumerate(tiles):
+                w_mx[um] = (wc[:, i * P : (i + 1) * P], ws[:, i * P : (i + 1) * P])
 
-        def second(u):
-            half, h = units[u]
+        place = {}
+
+        def second(*tiles):
             vc, vs = v_mx[0]
-            y_ps[u] = ps.tile([P, TILES, E], F32, name="y_bank", tag="y", bufs=2)
-            for m in range(TILES):
+            bank = ps.tile([P, len(tiles), E], F32, name="y_bank", tag="y", bufs=4)
+            name = "%d_%d" % tiles[0]
+            den_t = tile("den" + name, [P, len(tiles)], F32)
+            rden_t = tile("rden" + name, [P, len(tiles)], F32)
+            for i, (u, m) in enumerate(tiles):
+                h = units[u][1]
                 wc, ws = w_mx[u, m]
+                place[u, m] = (bank, den_t, rden_t, i)
                 nc.tensor.matmul_mx(
-                    out=y_ps[u][:, m, :],
-                    lhsT=wc[:].bitcast(FP8X4),
-                    lhsT_scale=ws[:],
+                    out=bank[:, i, :],
+                    lhsT=wc.bitcast(FP8X4),
+                    lhsT_scale=ws,
                     rhs=vc[:, h * E : (h + 1) * E].bitcast(FP8X4),
                     rhs_scale=vs[:, h * E : (h + 1) * E],
                     start=True,
                     stop=True,
                 )
 
-        def den_add(u):
-            nc.vector.tensor_scalar(out=den[u][:], in0=y_ps[u][:, :, E - 1], scalar1=1.0, scalar2=None, op0=ALU.add)
+        def den_add(u, m, eng):
+            bank, den_t, rden_t, i = place[u, m]
+            if eng is S:
+                nc.scalar.activation(out=den_t[:], in_=bank[:, :, E - 1], func=ACT.Copy, bias=1.0)
+            else:
+                nc.vector.tensor_scalar(out=den_t[:], in0=bank[:, :, E - 1], scalar1=1.0, scalar2=None, op0=ALU.add)
 
-        def den_recip(u):
-            nc.vector.reciprocal(out=rden[u][:], in_=den[u][:])
+        def den_recip(u, m):
+            bank, den_t, rden_t, i = place[u, m]
+            nc.vector.reciprocal(out=rden_t[:], in_=den_t[:])
 
-        def finish(u, m, queue):
-            half, h = units[u]
+        def finish(u, m):
+            bank, den_t, rden_t, i = place[u, m]
             nc.vector.scalar_tensor_tensor(
-                out=res[u][m][:], in0=y_ps[u][:, m, :], scalar=rden[u][:, m : m + 1],
+                out=res[u][:, m * E : (m + 1) * E], in0=bank[:, i, :], scalar=rden_t[:, i : i + 1],
                 in1=gate[u][:, m * E : (m + 1) * E], op0=ALU.mult, op1=ALU.mult,
             )
-            queue.dma_start(out=og_rows(out, u)[:, m * E : (m + 1) * E], in_=res[u][m][:])
+
+        def store(u, m0, m1, queue):
+            queue.dma_start(out=og_rows(out, u)[:, m0 * E : m1 * E], in_=res[u][:, m0 * E : m1 * E])
 
         v_mx = []
-        sigmoid(0)
-        group_k(0, nc.vector.tensor_copy)
-        group_k(1, nc.scalar.copy)
-        k_mx[0] = quantize("k0", k_grouped[0][:])
-        group_q(0, 0, Q_SPLIT, nc.vector.tensor_copy)
-        group_q(0, Q_SPLIT, P, nc.scalar.copy)
-        k_mx[1] = quantize("k1", k_grouped[1][:])
-        q_mx[0] = quantize("q0", q_grouped[0][:])
-        for r in range(PACK): scores(0, r)
-        group_q(1, 0, P, nc.vector.tensor_copy)
+        sigmoid(0, 0, 1)
+        group_k(0, V)
+        group_k(1, S)
+        quant_k(0)
+        group_q(0, V, 0, 88)
+        group_q(0, S, 88, 128)
+        quant_k(1)
+        quant_q(0)
+        full_scores(0)
+        full_scores(1)
+        full_rect(0)
+        full_rect(1)
         group_v(0)
-        q_mx[1] = quantize("q1", q_grouped[1][:])
         group_v(1)
-        for r in range(PACK): scores(1, r)
-        square(0, 0, False)
-        v_mx.append(quantize("v", v_grouped[:]))
-        square(0, 1, False)
-        quant_w(0, 0)
-        for r in range(PACK): scores(2, r)
-        square(1, 0, False)
-        quant_w(0, 1)
-        second(0)
-        square(1, 1, False)
-        quant_w(1, 0)
+        group_q(1, V)
+        quant_v()
+        quant_q(1)
+        full_scores(2)
+        full_scores(3)
+        full_rect(2)
+        full_rect(3)
+        square(0, 0, V)
+        square(0, 1, V)
+        square(1, 0, V)
+        quant_w((0, 0), (0, 1))
+        second((0, 0), (0, 1))
+        square(1, 1, V)
+        square(2, 0, V)
+        quant_w((1, 0), (1, 1))
+        second((1, 0), (1, 1))
+        den_add(0, 0, S)
+        sigmoid(0, 1, 2)
+        square(3, 0, S)
+        den_add(1, 0, S)
+        square(3, 1, S)
+        square(2, 1, V)
+        den_recip(0, 0)
+        quant_w((2, 0), (2, 1))
+        second((2, 0), (2, 1))
+        den_recip(1, 0)
+        finish(0, 0)
+        finish(0, 1)
+        store(0, 0, 2, nc.sync)
+        quant_w((3, 0), (3, 1))
+        second((3, 0), (3, 1))
         sigmoid(1)
-        den_add(0)
-        quant_w(1, 1)
-        den_recip(0)
-        for r in range(PACK): scores(3, r)
-        second(1)
-        square(2, 0, False)
-        finish(0, 0, nc.sync)
-        finish(0, 1, nc.sync)
-        square(2, 1, True)
-        den_add(1)
-        quant_w(2, 0)
-        den_recip(1)
-        square(3, 0, True)
-        quant_w(2, 1)
-        second(2)
-        finish(1, 0, nc.sync)
-        finish(1, 1, nc.sync)
-        square(3, 1, True)
+        den_add(2, 0, S)
         sigmoid(2)
         sigmoid(3)
-        den_add(2)
-        quant_w(3, 0)
-        den_recip(2)
-        quant_w(3, 1)
-        second(3)
-        finish(2, 0, nc.sync)
-        finish(2, 1, nc.sync)
-        den_add(3)
-        den_recip(3)
-        finish(3, 0, nc.sync)
-        finish(3, 1, nc.scalar)
+        den_add(3, 0, S)
+        finish(1, 0)
+        den_recip(2, 0)
+        finish(1, 1)
+        store(1, 0, 2, nc.sync)
+        finish(2, 0)
+        den_recip(3, 0)
+        finish(2, 1)
+        store(2, 0, 2, nc.sync)
+        finish(3, 0)
+        store(3, 0, 1, nc.scalar)
+        finish(3, 1)
+        store(3, 1, 2, nc.sync)

@@ -15,265 +15,260 @@ ALU = mybir.AluOpType
 
 P = 128
 PACK = 4
-ROWS = D // PACK
-HALF = NQ // 2
-TILES = HALF // P
-Q_SPLIT = 88
+HEAD_ROWS = D // PACK
+PAIR = 2
+CHUNK_TILES = (1, 2, 1)
+SHARED_TILE_VECTOR_PAIRS = 32
 
 
 def tile_rows_a_relu2_kb_gate_kernel(tc, qT, kT, t, v, kb, og, out):
     nc = tc.nc
+    chunks = range(len(CHUNK_TILES))
+    units = [(c, h) for c in chunks for h in range(H)]
+    first, middle, last = ([[(c, h, m) for m in range(CHUNK_TILES[c])] for h in range(H)] for c in chunks)
+    w_batches = [first[0] + first[1], middle[0], middle[1], last[0], last[1]]
+    y_groups = [first[0] + first[1] + middle[0], middle[1] + last[0], last[1]]
+
     with ExitStack() as ctx:
         sb = ctx.enter_context(tc.tile_pool(name="sb", bufs=1))
         ps = ctx.enter_context(tc.psum_pool(name="ps", bufs=1))
         ctx.enter_context(tc.manual_schedule())
 
-        def tile(name, shape, dtype):
+        def sbuf(name, shape, dtype):
             return sb.tile(shape, dtype, name=name, align_bytes=64)
 
         def quantize(name, grouped):
             width = grouped.shape[1] // PACK
-            codes = tile(name + "_codes", [P, width], U32)
-            scales = tile(name + "_scales", [P, width], U8)
-            nc.vector.quantize_mx(out=codes[:].bitcast(FP8X4), scales=scales[:], in_=grouped)
+            codes = sbuf(name + "_codes", [P, width], U32)
+            scales = sbuf(name + "_scales", [P, width], U8)
+            nc.vector.quantize_mx(out=codes[:].bitcast(FP8X4), scales=scales[:], in_=grouped[:])
             return codes, scales
 
-        units = [(half, h) for half in range(2) for h in range(H)]
+        def matmul(dst, lhs, rhs, rows, lhs_cols, rhs_cols):
+            nc.tensor.matmul_mx(
+                out=dst,
+                lhsT=lhs[0][rows, lhs_cols].bitcast(FP8X4),
+                lhsT_scale=lhs[1][rows, lhs_cols],
+                rhs=rhs[0][rows, rhs_cols].bitcast(FP8X4),
+                rhs_scale=rhs[1][rows, rhs_cols],
+                start=True,
+                stop=True,
+            )
 
-        t_sb = tile("t_sb", [P, PACK], F32)
-        kb_sb = tile("kb_sb", [P, PACK], F32)
-        og_sb = [tile("og_sb%d" % u, [P, TILES * E], F32) for u in range(len(units))]
-        k_raw = tile("k_raw", [P, PACK, N], F32)
-        q_raw = [tile("q_raw%d" % half, [P, PACK, HALF], F32) for half in range(2)]
-        v_raw = tile("v_raw", [P, H, PACK * E], F32)
+        def block(i, width=P):
+            return slice(i * width, (i + 1) * width)
 
-        def og_rows(ap, u):
-            half, h = units[u]
-            return ap[h, half * HALF : (half + 1) * HALF, :].rearrange("(p m) e -> p (m e)", m=TILES)
+        def queries(c):
+            return slice(P * sum(CHUNK_TILES[:c]), P * sum(CHUNK_TILES[: c + 1]))
 
-        q_view = qT.rearrange("h (p j) n -> (h p) j n", j=PACK)
-        nc.sync.dma_start(out=t_sb[:], in_=t.rearrange("(p j) o -> p (j o)", j=PACK))
-        og_first = tile("og_first", [P, E], F32)
-        nc.scalar.dma_start(out=og_first[:], in_=og_rows(og, 0)[:, :E])
-        nc.scalar.dma_start(out=kb_sb[:], in_=kb.rearrange("(p j) o -> p (j o)", j=PACK))
+        def chunk_rows(ap, c):
+            return ap[:, queries(c), :].rearrange("h (p m) e -> p h (m e)", p=P)
+
+        t_sb = sbuf("t_sb", [P, PACK], F32)
+        kb_sb = sbuf("kb_sb", [P, PACK], F32)
+        k_raw = sbuf("k_raw", [P, PACK, N], F32)
+        q_raw = [sbuf("q_raw%d" % c, [P, PACK, P * CHUNK_TILES[c]], F32) for c in chunks]
+        v_raw = sbuf("v_raw", [P, H, PACK * E], F32)
+        og_sb = {(c, h): sbuf("og_sb%d%d" % (c, h), [P, CHUNK_TILES[c] * E], F32) for c, h in units}
+
+        def load_q(c):
+            nc.sync.dma_start(out=q_raw[c][:], in_=qT.rearrange("h (p j) n -> (h p) j n", j=PACK)[:, :, queries(c)])
+
+        def load_og(unit, queue):
+            queue.dma_start(out=og_sb[unit][:], in_=chunk_rows(og, unit[0])[:, unit[1], :])
+
+        nc.sync.dma_start(out=t_sb[:], in_=t.rearrange("(p r) o -> p (r o)", r=PACK))
+        load_og(units[0], nc.scalar)
+        nc.scalar.dma_start(out=kb_sb[:], in_=kb.rearrange("(p r) o -> p (r o)", r=PACK))
         nc.sync.dma_start(out=k_raw[:], in_=kT.rearrange("h (p j) n -> (h p) j n", j=PACK))
-        nc.sync.dma_start(out=q_raw[0][:], in_=q_view[:, :, :HALF])
-        nc.sync.dma_start(out=v_raw[:], in_=v.rearrange("h (p j) e -> p h (j e)", j=PACK))
-        nc.sync.dma_start(out=q_raw[1][:], in_=q_view[:, :, HALF:])
-        nc.sync.dma_start(out=og_sb[0][:, E:], in_=og_rows(og, 0)[:, E:])
-        for u in range(1, len(units)):
-            nc.sync.dma_start(out=og_sb[u][:], in_=og_rows(og, u))
+        load_q(0)
+        load_q(1)
+        nc.sync.dma_start(out=v_raw[:], in_=v.rearrange("h (p r) e -> p h (r e)", r=PACK))
+        load_q(2)
+        for unit in units[1:]:
+            load_og(unit, nc.sync)
 
-        half_const = tile("half_const", [P, PACK], F32)
-        nc.gpsimd.memset(half_const[:], 0.5)
-        t_abs = tile("t_abs", [P, PACK], F32)
-        t_pos = tile("t_pos", [P, PACK], F32)
-        t_sign = tile("t_sign", [P, PACK], F32)
-        root = tile("root", [P, PACK], F32)
-        root_kb = tile("root_kb", [P, PACK], F32)
+        one_half = sbuf("one_half", [P, PACK], F32)
+        t_abs = sbuf("t_abs", [P, PACK], F32)
+        t_step = sbuf("t_step", [P, PACK], F32)
+        t_sign = sbuf("t_sign", [P, PACK], F32)
+        root = sbuf("root", [P, PACK], F32)
+        root_kb = sbuf("root_kb", [P, PACK], F32)
+        nc.gpsimd.memset(one_half[:], 0.5)
         nc.vector.scalar_tensor_tensor(out=t_abs[:], in0=t_sb[:], scalar=-1.0, in1=t_sb[:], op0=ALU.mult, op1=ALU.max)
-        nc.vector.tensor_scalar(out=t_pos[:], in0=t_sb[:], scalar1=0.0, scalar2=2.0, op0=ALU.is_ge, op1=ALU.mult)
-        nc.vector.tensor_scalar(out=t_sign[:], in0=t_pos[:], scalar1=-1.0, scalar2=None, op0=ALU.add)
-        nc.gpsimd.tensor_tensor(out=root[:], in0=t_abs[:], in1=half_const[:], op=ALU.pow)
+        nc.vector.tensor_scalar(out=t_step[:], in0=t_sb[:], scalar1=0.0, scalar2=2.0, op0=ALU.is_ge, op1=ALU.mult)
+        nc.vector.tensor_scalar(out=t_sign[:], in0=t_step[:], scalar1=-1.0, scalar2=None, op0=ALU.add)
+        nc.gpsimd.tensor_tensor(out=root[:], in0=t_abs[:], in1=one_half[:], op=ALU.pow)
         nc.gpsimd.tensor_tensor(out=root_kb[:], in0=root[:], in1=kb_sb[:], op=ALU.mult)
 
-        gate = [tile("gate%d" % u, [P, TILES * E], F32) for u in range(len(units))]
-
-        def sigmoid(u, m0=0, m1=TILES):
-            src = og_first[:] if m1 == 1 else og_sb[u][:, m0 * E : m1 * E]
-            nc.scalar.activation(out=gate[u][:, m0 * E : m1 * E], in_=src, func=ACT.Sigmoid)
-
-        V, S = nc.vector.tensor_copy, nc.scalar.copy
-
-        k_grouped = [tile("k_grouped%d" % rp, [P, 2 * P * PACK], BF16) for rp in range(2)]
+        k_grouped = [sbuf("k_grouped%d" % rp, [P, PAIR * P * PACK], BF16) for rp in range(PACK // PAIR)]
+        q_grouped = [sbuf("q_grouped%d" % c, [P, CHUNK_TILES[c] * P * PACK], BF16) for c in chunks]
+        v_grouped = sbuf("v_grouped", [P, H * E * PACK], BF16)
+        w_grouped = [sbuf("w_grouped%d" % b, [P, len(batch) * P * PACK], BF16) for b, batch in enumerate(w_batches)]
+        w_place = {tile: (b, i) for b, batch in enumerate(w_batches) for i, tile in enumerate(batch)}
+        y_place = {tile: (g, i) for g, group in enumerate(y_groups) for i, tile in enumerate(group)}
+        gate = {(c, h): sbuf("gate%d%d" % (c, h), [P, CHUNK_TILES[c] * E], F32) for c, h in units}
+        rect = {(c, h): sbuf("rect%d%d" % (c, h), [P, PACK, CHUNK_TILES[c] * P], F32) for c, h in units}
+        den = [sbuf("den%d" % g, [P, len(group)], F32) for g, group in enumerate(y_groups)]
+        inv_den = [sbuf("inv_den%d" % g, [P, len(group)], F32) for g, group in enumerate(y_groups)]
+        result = [sbuf("result%d" % c, [P, H, CHUNK_TILES[c] * E], F32) for c in chunks]
+        k_mx, q_mx, w_mx, score_banks, y_banks = {}, {}, {}, {}, {}
 
         def group_k(rp, copy):
             copy(
-                out=k_grouped[rp][:].rearrange("p (r s j) -> p s j r", r=2, j=PACK),
-                in_=k_raw[:].rearrange("p j (s r) -> p s j r", r=PACK)[:, :, :, 2 * rp : 2 * rp + 2],
+                out=k_grouped[rp][:].rearrange("p (r s j) -> p s j r", r=PAIR, j=PACK),
+                in_=k_raw[:].rearrange("p j (s r) -> p s j r", r=PACK)[:, :, :, block(rp, PAIR)],
             )
 
-        q_grouped = [tile("q_grouped%d" % half, [P, HALF * PACK], BF16) for half in range(2)]
-
-        def group_q(half, copy, s0=0, s1=P):
-            copy(
-                out=q_grouped[half][:].rearrange("p (m s j) -> p s j m", m=TILES, j=PACK)[:, s0:s1],
-                in_=q_raw[half][:].rearrange("p j (s m) -> p s j m", m=TILES)[:, s0:s1],
+        def group_q(c):
+            order = "p (i s j) -> p s j i" if CHUNK_TILES[c] == PAIR else "p (s i j) -> p s j i"
+            nc.vector.tensor_copy(
+                out=q_grouped[c][:].rearrange(order, i=PAIR, j=PACK),
+                in_=q_raw[c][:].rearrange("p j (s i) -> p s j i", i=PAIR),
             )
-
-        v_grouped = tile("v_grouped", [P, H * E * PACK], BF16)
 
         def group_v(h):
             nc.vector.tensor_tensor(
-                out=v_grouped[:, h * E * PACK : (h + 1) * E * PACK].rearrange("p (c i j) -> p c j i", i=2, j=PACK),
-                in0=v_raw[:, h, :].rearrange("p (j c i) -> p c j i", i=2, j=PACK),
-                in1=t_sign[:].unsqueeze(1).unsqueeze(3).to_broadcast([P, E // 2, PACK, 2]),
+                out=v_grouped[:, block(h, E * PACK)].rearrange("p (s i r) -> p s r i", i=PAIR, r=PACK),
+                in0=v_raw[:, h, :].rearrange("p (r s i) -> p s r i", i=PAIR, r=PACK),
+                in1=t_sign[:].unsqueeze(1).unsqueeze(3).to_broadcast([P, E // PAIR, PACK, PAIR]),
                 op=ALU.mult,
             )
 
-        k_mx = {}
-        q_mx = {}
-        w_mx = {}
-        rect = [tile("rect%d" % u, [P, PACK, HALF], F32) for u in range(len(units))]
-        w_grouped = [tile("w_grouped%d" % u, [P, TILES * P * PACK], BF16) for u in range(len(units))]
-        res = [tile("res%d" % u, [P, TILES * E], F32) for u in range(len(units))]
+        def square_views(tile, pairs):
+            c, h, m = tile
+            b, i = w_place[tile]
+            src = rect[c, h][:, :, block(m)].rearrange("p r (s i) -> p s r i", i=PAIR)
+            dst = w_grouped[b][:, block(i, P * PACK)].rearrange("p (s i r) -> p s r i", i=PAIR, r=PACK)
+            return src[:, pairs], dst[:, pairs]
 
-        banks = {}
+        def square_on_vector(tile, pairs=slice(None)):
+            src, dst = square_views(tile, pairs)
+            nc.vector.tensor_tensor(out=dst, in0=src, in1=src, op=ALU.mult)
 
-        def full_scores(u):
-            half, h = units[u]
-            rows = slice(h * ROWS, (h + 1) * ROWS)
-            qc, qs = q_mx[half]
-            for rp in range(2):
-                kc, ks = k_mx[rp]
-                banks[u, rp] = ps.tile([P, 2, HALF], F32, name="score_bank", tag="score%d" % h, bufs=2)
-                for i in range(2):
-                    kcols = slice(i * P, (i + 1) * P)
-                    for m in range(TILES):
-                        qcols = slice(m * P, (m + 1) * P)
-                        nc.tensor.matmul_mx(
-                            out=banks[u, rp][:, i, qcols],
-                            lhsT=kc[rows, kcols].bitcast(FP8X4),
-                            lhsT_scale=ks[rows, kcols],
-                            rhs=qc[rows, qcols].bitcast(FP8X4),
-                            rhs_scale=qs[rows, qcols],
-                            start=True,
-                            stop=True,
-                        )
+        def square_on_scalar(tile, pairs=slice(None)):
+            src, dst = square_views(tile, pairs)
+            nc.scalar.activation(out=dst, in_=src, func=ACT.Square)
 
-        def full_rect(u):
-            for r in range(PACK):
-                nc.scalar.activation(
-                    out=rect[u][:, r, :], in_=banks[u, r // 2][:, r % 2, :], func=ACT.Relu,
-                    bias=root_kb[:, r : r + 1], scale=root[:, r : r + 1],
-                )
+        def sigmoid(unit):
+            nc.scalar.activation(out=gate[unit][:], in_=og_sb[unit][:], func=ACT.Sigmoid)
 
-        def quant_k(rp):
-            k_mx[rp] = quantize("k%d" % rp, k_grouped[rp][:])
+        def scores(c):
+            for h in range(H):
+                for rp in range(PACK // PAIR):
+                    bank = ps.tile([P, PAIR, CHUNK_TILES[c] * P], F32, name="score_bank", tag="score%d" % h, bufs=2)
+                    score_banks[c, h, rp] = bank
+                    for i in range(PAIR):
+                        for m in range(CHUNK_TILES[c]):
+                            matmul(bank[:, i, block(m)], k_mx[rp], q_mx[c], block(h, HEAD_ROWS), block(i), block(m))
 
-        def quant_q(half):
-            q_mx[half] = quantize("q%d" % half, q_grouped[half][:])
+        def rectify(c):
+            for h in range(H):
+                for r in range(PACK):
+                    nc.scalar.activation(
+                        out=rect[c, h][:, r, :],
+                        in_=score_banks[c, h, r // PAIR][:, r % PAIR, :],
+                        func=ACT.Relu,
+                        bias=root_kb[:, r : r + 1],
+                        scale=root[:, r : r + 1],
+                    )
 
-        def quant_v():
-            v_mx.append(quantize("v", v_grouped[:]))
+        def quantize_w(b):
+            w_mx[b] = quantize("w%d" % b, w_grouped[b])
 
-        def square(u, m, eng):
-            src = rect[u][:, :, m * P : (m + 1) * P].rearrange("p r (c i) -> p c r i", i=2)
-            dst = w_grouped[u][:, m * P * PACK : (m + 1) * P * PACK].rearrange("p (c i r) -> p c r i", i=2, r=PACK)
-            if eng is S:
-                nc.scalar.activation(out=dst, in_=src, func=ACT.Square)
-            else:
-                nc.vector.tensor_tensor(out=dst, in0=src, in1=src, op=ALU.mult)
+        def second_product(g):
+            y_banks[g] = ps.tile([P, len(y_groups[g]), E], F32, name="y_bank", tag="y", bufs=len(y_groups))
+            for i, tile in enumerate(y_groups[g]):
+                b, column = w_place[tile]
+                matmul(y_banks[g][:, i, :], w_mx[b], v_mx, slice(0, P), block(column), block(tile[1], E))
 
-        def quant_w(*tiles):
-            u, m0 = tiles[0]
-            wc, ws = quantize("w%d_%d" % (u, m0), w_grouped[u][:, m0 * P * PACK : (m0 + len(tiles)) * P * PACK])
-            for i, um in enumerate(tiles):
-                w_mx[um] = (wc[:, i * P : (i + 1) * P], ws[:, i * P : (i + 1) * P])
+        def denominators_on_vector(g):
+            nc.vector.tensor_scalar(out=den[g][:], in0=y_banks[g][:, :, E - 1], scalar1=1.0, scalar2=None, op0=ALU.add)
 
-        place = {}
+        def denominators_on_scalar(g):
+            nc.scalar.activation(out=den[g][:], in_=y_banks[g][:, :, E - 1], func=ACT.Copy, bias=1.0)
 
-        def second(*tiles):
-            vc, vs = v_mx[0]
-            bank = ps.tile([P, len(tiles), E], F32, name="y_bank", tag="y", bufs=4)
-            name = "%d_%d" % tiles[0]
-            den_t = tile("den" + name, [P, len(tiles)], F32)
-            rden_t = tile("rden" + name, [P, len(tiles)], F32)
-            for i, (u, m) in enumerate(tiles):
-                h = units[u][1]
-                wc, ws = w_mx[u, m]
-                place[u, m] = (bank, den_t, rden_t, i)
-                nc.tensor.matmul_mx(
-                    out=bank[:, i, :],
-                    lhsT=wc.bitcast(FP8X4),
-                    lhsT_scale=ws,
-                    rhs=vc[:, h * E : (h + 1) * E].bitcast(FP8X4),
-                    rhs_scale=vs[:, h * E : (h + 1) * E],
-                    start=True,
-                    stop=True,
-                )
+        def invert(g):
+            nc.vector.reciprocal(out=inv_den[g][:], in_=den[g][:])
 
-        def den_add(u, m, eng):
-            bank, den_t, rden_t, i = place[u, m]
-            if eng is S:
-                nc.scalar.activation(out=den_t[:], in_=bank[:, :, E - 1], func=ACT.Copy, bias=1.0)
-            else:
-                nc.vector.tensor_scalar(out=den_t[:], in0=bank[:, :, E - 1], scalar1=1.0, scalar2=None, op0=ALU.add)
-
-        def den_recip(u, m):
-            bank, den_t, rden_t, i = place[u, m]
-            nc.vector.reciprocal(out=rden_t[:], in_=den_t[:])
-
-        def finish(u, m):
-            bank, den_t, rden_t, i = place[u, m]
+        def finish(tile):
+            c, h, m = tile
+            g, i = y_place[tile]
             nc.vector.scalar_tensor_tensor(
-                out=res[u][:, m * E : (m + 1) * E], in0=bank[:, i, :], scalar=rden_t[:, i : i + 1],
-                in1=gate[u][:, m * E : (m + 1) * E], op0=ALU.mult, op1=ALU.mult,
+                out=result[c][:, h, block(m, E)],
+                in0=y_banks[g][:, i, :],
+                scalar=inv_den[g][:, i : i + 1],
+                in1=gate[c, h][:, block(m, E)],
+                op0=ALU.mult,
+                op1=ALU.mult,
             )
 
-        def store(u, m0, m1, queue):
-            queue.dma_start(out=og_rows(out, u)[:, m0 * E : m1 * E], in_=res[u][:, m0 * E : m1 * E])
+        def store(c, heads, queue):
+            queue.dma_start(out=chunk_rows(out, c)[:, heads, :], in_=result[c][:, heads, :])
 
-        v_mx = []
-        sigmoid(0, 0, 1)
-        group_k(0, V)
-        group_k(1, S)
-        quant_k(0)
-        group_q(0, V, 0, 88)
-        group_q(0, S, 88, 128)
-        quant_k(1)
-        quant_q(0)
-        full_scores(0)
-        full_scores(1)
-        full_rect(0)
-        full_rect(1)
-        group_v(0)
-        group_v(1)
-        group_q(1, V)
-        quant_v()
-        quant_q(1)
-        full_scores(2)
-        full_scores(3)
-        full_rect(2)
-        full_rect(3)
-        square(0, 0, V)
-        square(0, 1, V)
-        square(1, 0, V)
-        quant_w((0, 0), (0, 1))
-        second((0, 0), (0, 1))
-        square(1, 1, V)
-        square(2, 0, V)
-        quant_w((1, 0), (1, 1))
-        second((1, 0), (1, 1))
-        den_add(0, 0, S)
-        sigmoid(0, 1, 2)
-        square(3, 0, S)
-        den_add(1, 0, S)
-        square(3, 1, S)
-        square(2, 1, V)
-        den_recip(0, 0)
-        quant_w((2, 0), (2, 1))
-        second((2, 0), (2, 1))
-        den_recip(1, 0)
-        finish(0, 0)
-        finish(0, 1)
-        store(0, 0, 2, nc.sync)
-        quant_w((3, 0), (3, 1))
-        second((3, 0), (3, 1))
-        sigmoid(1)
-        den_add(2, 0, S)
-        sigmoid(2)
-        sigmoid(3)
-        den_add(3, 0, S)
-        finish(1, 0)
-        den_recip(2, 0)
-        finish(1, 1)
-        store(1, 0, 2, nc.sync)
-        finish(2, 0)
-        den_recip(3, 0)
-        finish(2, 1)
-        store(2, 0, 2, nc.sync)
-        finish(3, 0)
-        store(3, 0, 1, nc.scalar)
-        finish(3, 1)
-        store(3, 1, 2, nc.sync)
+        sigmoid(units[0])
+        group_k(0, nc.vector.tensor_copy)
+        group_k(1, nc.scalar.copy)
+        group_q(0)
+        k_mx[0] = quantize("k0", k_grouped[0])
+        q_mx[0] = quantize("q0", q_grouped[0])
+        k_mx[1] = quantize("k1", k_grouped[1])
+        scores(0)
+        rectify(0)
+
+        group_q(1)
+        q_mx[1] = quantize("q1", q_grouped[1])
+        scores(1)
+        square_on_scalar(first[0][0])
+        rectify(1)
+
+        for h in range(H):
+            group_v(h)
+        group_q(2)
+        v_mx = quantize("v", v_grouped)
+        q_mx[2] = quantize("q2", q_grouped[2])
+        scores(2)
+        rectify(2)
+
+        shared = middle[1][1]
+        square_on_vector(first[1][0])
+        square_on_vector(middle[0][0])
+        quantize_w(0)
+        square_on_vector(middle[0][1])
+        square_on_vector(middle[1][0])
+        quantize_w(1)
+        second_product(0)
+        square_on_scalar(shared, slice(SHARED_TILE_VECTOR_PAIRS, None))
+        square_on_vector(shared, slice(0, SHARED_TILE_VECTOR_PAIRS))
+        square_on_scalar(last[0][0])
+        square_on_scalar(last[1][0])
+        quantize_w(2)
+        denominators_on_vector(0)
+        quantize_w(3)
+        second_product(1)
+        invert(0)
+        finish(first[0][0])
+        quantize_w(4)
+        second_product(2)
+
+        sigmoid(units[1])
+        sigmoid(units[2])
+        denominators_on_scalar(1)
+        sigmoid(units[3])
+        denominators_on_scalar(2)
+        sigmoid(units[4])
+        sigmoid(units[5])
+
+        finish(first[1][0])
+        store(0, slice(0, H), nc.sync)
+        for tile in middle[0]:
+            finish(tile)
+        store(1, slice(0, 1), nc.sync)
+        invert(1)
+        invert(2)
+        for tile in middle[1]:
+            finish(tile)
+        store(1, slice(1, 2), nc.sync)
+        for h, queue in enumerate((nc.scalar, nc.sync)):
+            finish(last[h][0])
+            store(2, slice(h, h + 1), queue)

@@ -235,18 +235,18 @@ def tile_rows_a_relu2_kb_gate_kernel(tc, qT, kT, t, v, kb, og, out):
         square_on_vector(middle[0][0])
         quantize_w(0)
         square_on_vector(middle[0][1])
-        square_on_vector(middle[1][0])
+        square_on_vector(shared, slice(0, SHARED_TILE_VECTOR_PAIRS))
         quantize_w(1)
         second_product(0)
+        square_on_vector(middle[1][0])
         square_on_scalar(shared, slice(SHARED_TILE_VECTOR_PAIRS, None))
-        square_on_vector(shared, slice(0, SHARED_TILE_VECTOR_PAIRS))
         square_on_scalar(last[0][0])
         square_on_scalar(last[1][0])
-        quantize_w(2)
         denominators_on_vector(0)
+        quantize_w(2)
+        invert(0)
         quantize_w(3)
         second_product(1)
-        invert(0)
         finish(first[0][0])
         quantize_w(4)
         second_product(2)
@@ -261,14 +261,11 @@ def tile_rows_a_relu2_kb_gate_kernel(tc, qT, kT, t, v, kb, og, out):
 
         finish(first[1][0])
         store(0, slice(0, H), nc.sync)
-        for tile in middle[0]:
-            finish(tile)
-        store(1, slice(0, 1), nc.sync)
-        invert(1)
-        invert(2)
-        for tile in middle[1]:
-            finish(tile)
-        store(1, slice(1, 2), nc.sync)
+        for h in range(H):
+            finish(middle[h][0])
+            invert(h + 1)
+            finish(middle[h][1])
+            store(1, slice(h, h + 1), nc.sync)
         for h, queue in enumerate((nc.scalar, nc.sync)):
             finish(last[h][0])
             store(2, slice(h, h + 1), queue)

from contextlib import ExitStack

import concourse.mybir as mybir

H, D, NQ, N, E = 2, 256, 512, 512, 128
FLOPS = 2 * H * NQ * N * (D + E)

F32 = mybir.dt.float32
BF16 = mybir.dt.bfloat16
U32 = mybir.dt.uint32
U8 = mybir.dt.uint8
FP8X4 = mybir.dt.float8_e4m3fn_x4
ACT = mybir.ActivationFunctionType
ALU = mybir.AluOpType

P = 128
PACK = 4
HEAD_ROWS = D // PACK
PAIR = 2
CHUNK_TILES = (1, 2, 1)
SHARED_TILE_VECTOR_PAIRS = 32


def tile_rows_a_relu2_kb_gate_kernel(tc, qT, kT, t, v, kb, og, out):
    nc = tc.nc
    chunks = range(len(CHUNK_TILES))
    units = [(c, h) for c in chunks for h in range(H)]
    first, middle, last = ([[(c, h, m) for m in range(CHUNK_TILES[c])] for h in range(H)] for c in chunks)
    w_batches = [first[0] + first[1], middle[0], middle[1], last[0], last[1]]
    y_groups = [first[0] + first[1] + middle[0], middle[1] + last[0], last[1]]

    with ExitStack() as ctx:
        sb = ctx.enter_context(tc.tile_pool(name="sb", bufs=1))
        ps = ctx.enter_context(tc.psum_pool(name="ps", bufs=1))
        ctx.enter_context(tc.manual_schedule())

        def sbuf(name, shape, dtype):
            return sb.tile(shape, dtype, name=name, align_bytes=64)

        def quantize(name, grouped):
            width = grouped.shape[1] // PACK
            codes = sbuf(name + "_codes", [P, width], U32)
            scales = sbuf(name + "_scales", [P, width], U8)
            nc.vector.quantize_mx(out=codes[:].bitcast(FP8X4), scales=scales[:], in_=grouped[:])
            return codes, scales

        def matmul(dst, lhs, rhs, rows, lhs_cols, rhs_cols):
            nc.tensor.matmul_mx(
                out=dst,
                lhsT=lhs[0][rows, lhs_cols].bitcast(FP8X4),
                lhsT_scale=lhs[1][rows, lhs_cols],
                rhs=rhs[0][rows, rhs_cols].bitcast(FP8X4),
                rhs_scale=rhs[1][rows, rhs_cols],
                start=True,
                stop=True,
            )

        def block(i, width=P):
            return slice(i * width, (i + 1) * width)

        def queries(c):
            return slice(P * sum(CHUNK_TILES[:c]), P * sum(CHUNK_TILES[: c + 1]))

        def chunk_rows(ap, c):
            return ap[:, queries(c), :].rearrange("h (p m) e -> p h (m e)", p=P)

        t_sb = sbuf("t_sb", [P, PACK], F32)
        kb_sb = sbuf("kb_sb", [P, PACK], F32)
        k_raw = sbuf("k_raw", [P, PACK, N], F32)
        q_raw = [sbuf("q_raw%d" % c, [P, PACK, P * CHUNK_TILES[c]], F32) for c in chunks]
        v_raw = sbuf("v_raw", [P, H, PACK * E], F32)
        og_sb = {(c, h): sbuf("og_sb%d%d" % (c, h), [P, CHUNK_TILES[c] * E], F32) for c, h in units}

        def load_q(c):
            nc.sync.dma_start(out=q_raw[c][:], in_=qT.rearrange("h (p j) n -> (h p) j n", j=PACK)[:, :, queries(c)])

        def load_og(unit, queue):
            queue.dma_start(out=og_sb[unit][:], in_=chunk_rows(og, unit[0])[:, unit[1], :])

        nc.sync.dma_start(out=t_sb[:], in_=t.rearrange("(p r) o -> p (r o)", r=PACK))
        load_og(units[0], nc.scalar)
        nc.scalar.dma_start(out=kb_sb[:], in_=kb.rearrange("(p r) o -> p (r o)", r=PACK))
        nc.sync.dma_start(out=k_raw[:], in_=kT.rearrange("h (p j) n -> (h p) j n", j=PACK))
        load_q(0)
        load_q(1)
        nc.sync.dma_start(out=v_raw[:], in_=v.rearrange("h (p r) e -> p h (r e)", r=PACK))
        load_q(2)
        for unit in units[1:]:
            load_og(unit, nc.sync)

        one_half = sbuf("one_half", [P, PACK], F32)
        t_abs = sbuf("t_abs", [P, PACK], F32)
        t_step = sbuf("t_step", [P, PACK], F32)
        t_sign = sbuf("t_sign", [P, PACK], F32)
        root = sbuf("root", [P, PACK], F32)
        root_kb = sbuf("root_kb", [P, PACK], F32)
        nc.gpsimd.memset(one_half[:], 0.5)
        nc.vector.scalar_tensor_tensor(out=t_abs[:], in0=t_sb[:], scalar=-1.0, in1=t_sb[:], op0=ALU.mult, op1=ALU.max)
        nc.vector.tensor_scalar(out=t_step[:], in0=t_sb[:], scalar1=0.0, scalar2=2.0, op0=ALU.is_ge, op1=ALU.mult)
        nc.vector.tensor_scalar(out=t_sign[:], in0=t_step[:], scalar1=-1.0, scalar2=None, op0=ALU.add)
        nc.gpsimd.tensor_tensor(out=root[:], in0=t_abs[:], in1=one_half[:], op=ALU.pow)
        nc.gpsimd.tensor_tensor(out=root_kb[:], in0=root[:], in1=kb_sb[:], op=ALU.mult)

        k_grouped = [sbuf("k_grouped%d" % rp, [P, PAIR * P * PACK], BF16) for rp in range(PACK // PAIR)]
        q_grouped = [sbuf("q_grouped%d" % c, [P, CHUNK_TILES[c] * P * PACK], BF16) for c in chunks]
        v_grouped = sbuf("v_grouped", [P, H * E * PACK], BF16)
        w_grouped = [sbuf("w_grouped%d" % b, [P, len(batch) * P * PACK], BF16) for b, batch in enumerate(w_batches)]
        w_place = {tile: (b, i) for b, batch in enumerate(w_batches) for i, tile in enumerate(batch)}
        y_place = {tile: (g, i) for g, group in enumerate(y_groups) for i, tile in enumerate(group)}
        gate = {(c, h): sbuf("gate%d%d" % (c, h), [P, CHUNK_TILES[c] * E], F32) for c, h in units}
        rect = {(c, h): sbuf("rect%d%d" % (c, h), [P, PACK, CHUNK_TILES[c] * P], F32) for c, h in units}
        den = [sbuf("den%d" % g, [P, len(group)], F32) for g, group in enumerate(y_groups)]
        inv_den = [sbuf("inv_den%d" % g, [P, len(group)], F32) for g, group in enumerate(y_groups)]
        result = [sbuf("result%d" % c, [P, H, CHUNK_TILES[c] * E], F32) for c in chunks]
        k_mx, q_mx, w_mx, score_banks, y_banks = {}, {}, {}, {}, {}

        def group_k(rp, copy):
            copy(
                out=k_grouped[rp][:].rearrange("p (r s j) -> p s j r", r=PAIR, j=PACK),
                in_=k_raw[:].rearrange("p j (s r) -> p s j r", r=PACK)[:, :, :, block(rp, PAIR)],
            )

        def group_q(c):
            order = "p (i s j) -> p s j i" if CHUNK_TILES[c] == PAIR else "p (s i j) -> p s j i"
            nc.vector.tensor_copy(
                out=q_grouped[c][:].rearrange(order, i=PAIR, j=PACK),
                in_=q_raw[c][:].rearrange("p j (s i) -> p s j i", i=PAIR),
            )

        def group_v(h):
            nc.vector.tensor_tensor(
                out=v_grouped[:, block(h, E * PACK)].rearrange("p (s i r) -> p s r i", i=PAIR, r=PACK),
                in0=v_raw[:, h, :].rearrange("p (r s i) -> p s r i", i=PAIR, r=PACK),
                in1=t_sign[:].unsqueeze(1).unsqueeze(3).to_broadcast([P, E // PAIR, PACK, PAIR]),
                op=ALU.mult,
            )

        def square_views(tile, pairs):
            c, h, m = tile
            b, i = w_place[tile]
            src = rect[c, h][:, :, block(m)].rearrange("p r (s i) -> p s r i", i=PAIR)
            dst = w_grouped[b][:, block(i, P * PACK)].rearrange("p (s i r) -> p s r i", i=PAIR, r=PACK)
            return src[:, pairs], dst[:, pairs]

        def square_on_vector(tile, pairs=slice(None)):
            src, dst = square_views(tile, pairs)
            nc.vector.tensor_tensor(out=dst, in0=src, in1=src, op=ALU.mult)

        def square_on_scalar(tile, pairs=slice(None)):
            src, dst = square_views(tile, pairs)
            nc.scalar.activation(out=dst, in_=src, func=ACT.Square)

        def sigmoid(unit):
            nc.scalar.activation(out=gate[unit][:], in_=og_sb[unit][:], func=ACT.Sigmoid)

        def scores(c):
            for h in range(H):
                for rp in range(PACK // PAIR):
                    bank = ps.tile([P, PAIR, CHUNK_TILES[c] * P], F32, name="score_bank", tag="score%d" % h, bufs=2)
                    score_banks[c, h, rp] = bank
                    for i in range(PAIR):
                        for m in range(CHUNK_TILES[c]):
                            matmul(bank[:, i, block(m)], k_mx[rp], q_mx[c], block(h, HEAD_ROWS), block(i), block(m))

        def rectify(c):
            for h in range(H):
                for r in range(PACK):
                    nc.scalar.activation(
                        out=rect[c, h][:, r, :],
                        in_=score_banks[c, h, r // PAIR][:, r % PAIR, :],
                        func=ACT.Relu,
                        bias=root_kb[:, r : r + 1],
                        scale=root[:, r : r + 1],
                    )

        def quantize_w(b):
            w_mx[b] = quantize("w%d" % b, w_grouped[b])

        def second_product(g):
            y_banks[g] = ps.tile([P, len(y_groups[g]), E], F32, name="y_bank", tag="y", bufs=len(y_groups))
            for i, tile in enumerate(y_groups[g]):
                b, column = w_place[tile]
                matmul(y_banks[g][:, i, :], w_mx[b], v_mx, slice(0, P), block(column), block(tile[1], E))

        def denominators_on_vector(g):
            nc.vector.tensor_scalar(out=den[g][:], in0=y_banks[g][:, :, E - 1], scalar1=1.0, scalar2=None, op0=ALU.add)

        def denominators_on_scalar(g):
            nc.scalar.activation(out=den[g][:], in_=y_banks[g][:, :, E - 1], func=ACT.Copy, bias=1.0)

        def invert(g):
            nc.vector.reciprocal(out=inv_den[g][:], in_=den[g][:])

        def finish(tile):
            c, h, m = tile
            g, i = y_place[tile]
            nc.vector.scalar_tensor_tensor(
                out=result[c][:, h, block(m, E)],
                in0=y_banks[g][:, i, :],
                scalar=inv_den[g][:, i : i + 1],
                in1=gate[c, h][:, block(m, E)],
                op0=ALU.mult,
                op1=ALU.mult,
            )

        def store(c, heads, queue):
            queue.dma_start(out=chunk_rows(out, c)[:, heads, :], in_=result[c][:, heads, :])

        sigmoid(units[0])
        group_k(0, nc.vector.tensor_copy)
        group_k(1, nc.scalar.copy)
        group_q(0)
        k_mx[0] = quantize("k0", k_grouped[0])
        q_mx[0] = quantize("q0", q_grouped[0])
        k_mx[1] = quantize("k1", k_grouped[1])
        scores(0)
        rectify(0)

        group_q(1)
        q_mx[1] = quantize("q1", q_grouped[1])
        scores(1)
        square_on_scalar(first[0][0])
        rectify(1)

        for h in range(H):
            group_v(h)
        group_q(2)
        v_mx = quantize("v", v_grouped)
        q_mx[2] = quantize("q2", q_grouped[2])
        scores(2)
        rectify(2)

        shared = middle[1][1]
        square_on_vector(first[1][0])
        square_on_vector(middle[0][0])
        quantize_w(0)
        square_on_vector(middle[0][1])
        square_on_vector(shared, slice(0, SHARED_TILE_VECTOR_PAIRS))
        quantize_w(1)
        second_product(0)
        square_on_vector(middle[1][0])
        square_on_scalar(shared, slice(SHARED_TILE_VECTOR_PAIRS, None))
        square_on_scalar(last[0][0])
        square_on_scalar(last[1][0])
        denominators_on_vector(0)
        quantize_w(2)
        invert(0)
        quantize_w(3)
        second_product(1)
        finish(first[0][0])
        quantize_w(4)
        second_product(2)

        sigmoid(units[1])
        sigmoid(units[2])
        denominators_on_scalar(1)
        sigmoid(units[3])
        denominators_on_scalar(2)
        sigmoid(units[4])
        sigmoid(units[5])

        finish(first[1][0])
        store(0, slice(0, H), nc.sync)
        for h in range(H):
            finish(middle[h][0])
            invert(h + 1)
            finish(middle[h][1])
            store(1, slice(h, h + 1), nc.sync)
        for h, queue in enumerate((nc.scalar, nc.sync)):
            finish(last[h][0])
            store(2, slice(h, h + 1), queue)
